import numpy as np
import ml_dtypes


def mxq(x, axis, fmt="e4m3"):
    dtype, down = {"e4m3": (ml_dtypes.float8_e4m3fn, 7), "e5m2": (ml_dtypes.float8_e5m2, 14)}[fmt]
    v = np.moveaxis(np.asarray(x, np.float32).astype(ml_dtypes.bfloat16).astype(np.float64), axis, -1)
    blocks = v.reshape(v.shape[:-1] + (-1, 32))
    amax = np.abs(blocks).max(-1, keepdims=True)
    byte = np.maximum(np.where(amax > 0, np.frexp(amax)[1] - 1 + 127, 0) - down, 1)
    scale = np.exp2(byte - 127.0)
    codes = (blocks / scale).astype(np.float32).astype(dtype).astype(np.float64)
    return np.moveaxis((codes * scale).reshape(v.shape), -1, axis)


WIDE = False


def mx_kscale(k):
    if not WIDE:
        return np.ones(k)
    levels = np.array([10, -10, 5, -5, 0])
    if k % 512:
        return np.exp2(np.random.permutation(np.resize(levels, k // 32))).repeat(32)
    a = np.empty((k // 512, 16))
    for p in range(k // 512):
        a[p, :8] = np.random.permutation(np.resize(levels, 8))
        for g in range(8):
            far = levels[np.abs(levels - a[p, g]) >= 10]
            a[p, g + 8] = far[np.random.randint(len(far))]
    return np.exp2(a.ravel()).repeat(32)


def f64(x):
    return np.asarray(x).astype(np.float64)


def striped(idx):
    return np.tile(np.asarray(idx).reshape(-1, 16).T, (8, 1)).astype(np.uint16)


def unstriped(offs):
    return offs[:16].T.reshape(-1).astype(np.int64)


E2M1 = np.array([0.0, 0.5, 1.0, 1.5, 2.0, 3.0, 4.0, 6.0, -0.0, -0.5, -1.0, -1.5, -2.0, -3.0, -4.0, -6.0])


def pack_weight(w, fmt):
    k, n = w.shape
    w = f64(np.asarray(w, np.float32).astype(ml_dtypes.bfloat16)).reshape(k // 32, 32, n)
    amax = np.abs(w).max(1)
    if fmt == "e4m3":
        byte = np.frexp(amax)[1] - 1 + 127 - 7
    else:
        mant, ex = np.frexp(amax / 6.0)
        byte = np.where(mant > 0.5, ex, ex - 1) + 127
    byte = np.clip(np.where(amax > 0, byte, 1), 1, 254)
    scaled = (w * np.exp2(127.0 - byte)[:, None, :]).reshape(k, n).astype(np.float32)
    by_word = np.ascontiguousarray(scaled.reshape(k // 512, 128, 4, n).transpose(0, 1, 3, 2))
    if fmt == "e4m3":
        words = by_word.astype(ml_dtypes.float8_e4m3fn).view(np.uint8)
    else:
        c = by_word.astype(ml_dtypes.float4_e2m1fn).view(np.uint8) & 0xF
        words = (c[..., 0::2] | (c[..., 1::2] << 4)).reshape(k // 512, 128, 2 * n)
    return np.ascontiguousarray(words), np.ascontiguousarray(byte.astype(np.uint8).reshape(k // 512, 16, n))


def unpack_weight(words, scales, fmt):
    g, _, n = scales.shape
    words = np.ascontiguousarray(words).reshape(g, 128, n, -1)
    if fmt == "e4m3":
        vals = words.view(ml_dtypes.float8_e4m3fn).astype(np.float64)
    else:
        nib = np.empty((g, 128, n, 4), np.uint8)
        nib[..., 0::2] = words & 0xF
        nib[..., 1::2] = words >> 4
        vals = E2M1[nib]
    vals = vals * np.repeat(np.exp2(scales.astype(np.float64) - 127.0), 8, axis=1)[..., None]
    return vals.transpose(0, 1, 3, 2).reshape(g * 512, n)


def softplus(v):
    return np.log(1.0 + np.exp(v))


def sigmoid(v):
    return 1.0 / (1.0 + np.exp(-v))


D, E, T, I, Q = 512, 512, 2048, 512, 128


def setup_inputs():
    n = np.random.standard_normal
    idx = np.random.permutation(T)[:I]
    fd = mx_kscale(D)
    fe = mx_kscale(E)
    keysp = pack_weight(n((D, T)) / fd[:, None], "e2m1")
    valsp = pack_weight(n((E, T)) / fe[:, None], "e2m1")
    return {
        "query": (n((D, Q)) * 0.6 / np.sqrt(D) * fd[:, None]).astype(np.float32),
        "query2": (n((D, Q)) * 1.0 / np.sqrt(D) * fd[:, None]).astype(np.float32),
        "keys_words": keysp[0],
        "keys_scales": keysp[1],
        "strict": (np.random.uniform(0.4, 1.2, (Q, 1))).astype(np.float32),
        "gout": (n((E, Q)) * 1 / np.sqrt(E) * fe[:, None]).astype(np.float32),
        "vals_words": valsp[0],
        "vals_scales": valsp[1],
        "old": (0.5 * n((Q, T))).astype(np.float32),
        "offs": striped(idx),
    }


def reference(query, query2, keys_words, keys_scales, strict, gout, vals_words, vals_scales, old, offs):
    idx = unstriped(offs)
    keysu = unpack_weight(keys_words, keys_scales, "e2m1")
    valsu = unpack_weight(vals_words, vals_scales, "e2m1")
    queryq = mxq(f64(query), 0, "e4m3")
    keysidxg = keysu[:, idx]
    a = queryq.T @ keysidxg
    query2q = mxq(f64(query2), 0, "e4m3")
    b = query2q.T @ keysidxg
    s = a - softplus(b) * f64(strict)
    p = np.exp(s - np.max(s, axis=1, keepdims=True))
    z = np.sum(p, axis=1, keepdims=True)
    goutq = mxq(f64(gout), 0, "e4m3")
    valsidxg = valsu[:, idx]
    c0 = goutq.T @ valsidxg
    dz = np.sum(c0 * p / np.square(z) * (-1.0), axis=1, keepdims=True)
    dp = c0 / z + dz
    ds = dp * p
    db = ds * (-1.0) * f64(strict) * sigmoid(b)
    gs = db * 512.0
    gf = np.zeros((Q, T))
    gf[:, idx] = gs
    y = f64(old) + gf
    return y

from contextlib import ExitStack

import concourse.mybir as mybir

D, T, SLOTS, Q = 512, 2048, 512, 128
FLOPS = 3 * 2 * D * SLOTS * Q

F32 = mybir.dt.float32
BF16 = mybir.dt.bfloat16
I32 = mybir.dt.int32
U32 = mybir.dt.uint32
U16 = mybir.dt.uint16
U8 = mybir.dt.uint8
FP8X4 = mybir.dt.float8_e4m3fn_x4
FP4X4 = mybir.dt.float4_e2m1fn_x4
ALU = mybir.AluOpType
ACT = mybir.ActivationFunctionType
AXIS = mybir.AxisListType

P = 128
PACK = 4
HALF = SLOTS // 2
LN_FLOOR = 2.0 ** -60
OUT_CHUNKS = (256, 512, 512, 512, 256)


def tile_attend_bheldback_s_kernel(tc, query, query2, keys_words, keys_scales, strict, gout,
                                    vals_words, vals_scales, old, offs, out):
    nc = tc.nc
    with ExitStack() as ctx:
        sb = ctx.enter_context(tc.tile_pool(name="sb", bufs=1))
        ps = ctx.enter_context(tc.psum_pool(name="ps", bufs=1))

        def tile(shape, dtype, name, tag=None):
            return sb.tile(shape, dtype, name=name, tag=tag or name, align_bytes=64)

        offsets = sb.tile([P, SLOTS // 16], U16, name="offsets")
        nc.sync.dma_start(offsets[:], offs)
        halves = [slice(h * HALF, (h + 1) * HALF) for h in range(2)]
        half_offsets = [offsets[:, h * HALF // 16:(h + 1) * HALF // 16] for h in range(2)]

        def load_scales(queue, scales, name):
            plane = tile([P, T], U8, name)
            nc.vector.memset(plane[:].bitcast(I32), 0)
            rows = scales[0].bitcast(I32)
            for quad in range(4):
                queue.dma_start(plane[32 * quad:32 * quad + 4, :].bitcast(I32), rows[4 * quad:4 * quad + 4, :])
            return plane

        def load_words(words, name, tag):
            pool_words = tile([P, T], U16, name, tag)
            nc.sync.dma_start(pool_words[:].bitcast(I32), words[0].bitcast(I32))
            return pool_words

        def load_rows(rows, name, tag):
            raw = tile([P, PACK, Q], F32, name, tag)
            nc.sync.dma_start(raw[:], rows.rearrange("(p j) q -> p j q", j=PACK))
            return raw

        def interleave(copy, raw, name):
            grouped = tile([P, Q, PACK], BF16, name)
            copy(grouped[:], raw[:].rearrange("p j q -> p q j"))
            return grouped

        def quantize(grouped, name):
            codes = tile([P, Q], U32, name + "_codes")
            scale = tile([P, Q], U8, name + "_scale")
            nc.vector.quantize_mx(out=codes[:].bitcast(FP8X4), scales=scale[:],
                                  in_=grouped[:].rearrange("p q j -> p (q j)"))
            return codes, scale

        def product(name, stationary, words, scale):
            acc = ps.tile([P, words.shape[1]], F32, name=name)
            nc.tensor.matmul_mx(out=acc[:], lhsT=stationary[0][:].bitcast(FP8X4), lhsT_scale=stationary[1][:],
                                rhs=words.bitcast(FP4X4), rhs_scale=scale, start=True, stop=True)
            return acc

        ks_plane = load_scales(nc.scalar, keys_scales, "ks_plane")
        warm = tile([P, 1], F32, "warm", "warm_then_vw")
        warm_out = tile([P, 1], F32, "warm_out", "warm_then_strict")
        nc.vector.memset(warm[:], 0.0)
        nc.scalar.activation(warm_out[:], warm[:], ACT.Sigmoid)
        q2_raw = load_rows(query2, "q2_raw", "q2_then_g")
        kw_pool = load_words(keys_words, "kw_pool", "kw_then_old")
        q_raw = load_rows(query, "q_raw", "q_raw")
        vw_pool = load_words(vals_words, "vw_pool", "warm_then_vw")
        vs_plane = load_scales(nc.sync, vals_scales, "vs_plane")
        strict_col = tile([P, 1], F32, "strict_col", "warm_then_strict")
        nc.sync.dma_start(strict_col[:], strict)

        gf = tile([P, T], F32, "gf")
        nc.vector.memset(gf[:], 0.0)

        ks = tile([P, SLOTS], U8, "ks")
        nc.vector.tensor_copy(ks[:], ks_plane[:].indirect(offsets[:]))
        q2_mx = quantize(interleave(nc.scalar.copy, q2_raw, "q2_bf"), "q2")
        g_raw = load_rows(gout, "g_raw", "q2_then_g")
        kw = tile([P, SLOTS], U16, "kw")
        b_ps = []
        keep = tile([P, SLOTS], F32, "keep")
        for h in range(2):
            nc.vector.tensor_copy(kw[:, halves[h]], kw_pool[:].indirect(half_offsets[h]))
            b_ps.append(product("b%d" % h, q2_mx, kw[:, halves[h]], ks[:, halves[h]]))
        old_sb = tile([P, T], F32, "old_sb", "kw_then_old")
        nc.sync.dma_start(old_sb[:], old)
        q_bf = interleave(nc.scalar.copy, q_raw, "q_bf")
        for h in range(2):
            nc.scalar.activation(keep[:, halves[h]], b_ps[h][:], ACT.Sigmoid, scale=-1.0)
        log_keep = tile([P, SLOTS], F32, "log_keep")
        for h in range(2):
            nc.scalar.activation(log_keep[:, halves[h]], keep[:, halves[h]], ACT.Ln, bias=LN_FLOOR)

        vs = tile([P, SLOTS], U8, "vs")
        nc.vector.tensor_copy(vs[:], vs_plane[:].indirect(offsets[:]))
        q_mx = quantize(q_bf, "q")
        a_ps = product("a", q_mx, kw[:], ks[:])
        vw = tile([P, SLOTS], U16, "vw")
        nc.vector.tensor_copy(vw[:], vw_pool[:].indirect(offsets[:]))
        g_bf = interleave(nc.vector.tensor_copy, g_raw, "g_bf")
        neg_scale = tile([P, 1], F32, "neg_scale")
        nc.vector.tensor_scalar(neg_scale[:], strict_col[:], -512.0, None, ALU.mult)
        g_mx = quantize(g_bf, "g")
        c_ps = product("c", g_mx, vw[:], vs[:])

        neg_sp = tile([P, SLOTS], F32, "neg_sp")
        for h in range(2):
            nc.vector.scalar_tensor_tensor(neg_sp[:, halves[h]], b_ps[h][:], -1.0, log_keep[:, halves[h]],
                                           ALU.mult, ALU.min)
        s = tile([P, SLOTS], F32, "s")
        for h in range(2):
            nc.vector.scalar_tensor_tensor(s[:, halves[h]], neg_sp[:, halves[h]], strict_col[:],
                                           a_ps[:, halves[h]], ALU.mult, ALU.add)
        neg_max = tile([P, 1], F32, "neg_max")
        nc.vector.tensor_reduce(neg_max[:], s[:], AXIS.X, ALU.max, negate=True)
        p = tile([P, SLOTS], F32, "p")
        z = tile([P, 1], F32, "z")
        nc.scalar.activation(p[:], s[:], ACT.Exp, bias=neg_max[:], accum_out=z[:])
        log_sig = tile([P, SLOTS], F32, "log_sig")
        for h in range(2):
            nc.vector.tensor_tensor(log_sig[:, halves[h]], b_ps[h][:], neg_sp[:, halves[h]], ALU.add)
        sig = tile([P, SLOTS], F32, "sig")
        nc.scalar.activation(sig[:], log_sig[:], ACT.Exp)

        z_inv = tile([P, 1], F32, "z_inv")
        nc.vector.reciprocal(z_inv[:], z[:])
        weighted = tile([P, SLOTS], F32, "weighted")
        mean_c = tile([P, 1], F32, "mean_c")
        nc.vector.scalar_tensor_tensor(weighted[:], c_ps[:], z_inv[:], p[:], ALU.mult, ALU.mult,
                                       accum_out=mean_c[:])
        row_scale = tile([P, 1], F32, "row_scale")
        nc.scalar.activation(row_scale[:], z_inv[:], ACT.Copy, scale=neg_scale[:])
        sig_scaled = tile([P, SLOTS], F32, "sig_scaled")
        nc.scalar.activation(sig_scaled[:], sig[:], ACT.Copy, scale=row_scale[:])
        centred = tile([P, SLOTS], F32, "centred")
        nc.vector.scalar_tensor_tensor(centred[:], c_ps[:], mean_c[:], p[:], ALU.subtract, ALU.mult)
        nc.vector.tensor_tensor(gf[:].indirect(offsets[:]), centred[:], sig_scaled[:], ALU.mult)

        start = 0
        for n, width in enumerate(OUT_CHUNKS):
            cols = slice(start, start + width)
            res = tile([P, width], F32, "res%d" % n)
            nc.vector.tensor_tensor(res[:], old_sb[:, cols], gf[:, cols], ALU.add)
            nc.sync.dma_start(out[:, cols], res[:])
            start = start + width
